import numpy as np
import ml_dtypes


def mxq(x, axis, fmt="e4m3"):
    dtype, down = {"e4m3": (ml_dtypes.float8_e4m3fn, 7), "e5m2": (ml_dtypes.float8_e5m2, 14)}[fmt]
    v = np.moveaxis(np.asarray(x, np.float32).astype(ml_dtypes.bfloat16).astype(np.float64), axis, -1)
    blocks = v.reshape(v.shape[:-1] + (-1, 32))
    amax = np.abs(blocks).max(-1, keepdims=True)
    byte = np.maximum(np.where(amax > 0, np.frexp(amax)[1] - 1 + 127, 0) - down, 1)
    scale = np.exp2(byte - 127.0)
    codes = (blocks / scale).astype(np.float32).astype(dtype).astype(np.float64)
    return np.moveaxis((codes * scale).reshape(v.shape), -1, axis)


WIDE = False


def mx_kscale(k):
    if not WIDE:
        return np.ones(k)
    levels = np.array([10, -10, 5, -5, 0])
    if k % 512:
        return np.exp2(np.random.permutation(np.resize(levels, k // 32))).repeat(32)
    a = np.empty((k // 512, 16))
    for p in range(k // 512):
        a[p, :8] = np.random.permutation(np.resize(levels, 8))
        for g in range(8):
            far = levels[np.abs(levels - a[p, g]) >= 10]
            a[p, g + 8] = far[np.random.randint(len(far))]
    return np.exp2(a.ravel()).repeat(32)


def f64(x):
    return np.asarray(x).astype(np.float64)


def striped(idx):
    return np.tile(idx.reshape(-1, 16).T, (8, 1)).astype(np.uint16)


def unstriped(offs):
    return offs[:16].T.reshape(-1).astype(np.int64)


E2M1 = np.array([0.0, 0.5, 1.0, 1.5, 2.0, 3.0, 4.0, 6.0, -0.0, -0.5, -1.0, -1.5, -2.0, -3.0, -4.0, -6.0])


def pack_weight(w, fmt):
    k, n = w.shape
    w = f64(np.asarray(w, np.float32).astype(ml_dtypes.bfloat16)).reshape(k // 32, 32, n)
    amax = np.abs(w).max(1)
    if fmt == "e4m3":
        byte = np.frexp(amax)[1] - 1 + 127 - 7
    else:
        mant, ex = np.frexp(amax / 6.0)
        byte = np.where(mant > 0.5, ex, ex - 1) + 127
    byte = np.clip(np.where(amax > 0, byte, 1), 1, 254)
    scaled = (w * np.exp2(127.0 - byte)[:, None, :]).reshape(k, n).astype(np.float32)
    by_word = np.ascontiguousarray(scaled.reshape(k // 512, 128, 4, n).transpose(0, 1, 3, 2))
    if fmt == "e4m3":
        words = by_word.astype(ml_dtypes.float8_e4m3fn).view(np.uint8)
    else:
        c = by_word.astype(ml_dtypes.float4_e2m1fn).view(np.uint8) & 0xF
        words = (c[..., 0::2] | (c[..., 1::2] << 4)).reshape(k // 512, 128, 2 * n)
    return np.ascontiguousarray(words), np.ascontiguousarray(byte.astype(np.uint8).reshape(k // 512, 16, n))


def unpack_weight(words, scales, fmt):
    g, _, n = scales.shape
    words = np.ascontiguousarray(words).reshape(g, 128, n, -1)
    if fmt == "e4m3":
        vals = words.view(ml_dtypes.float8_e4m3fn).astype(np.float64)
    else:
        nib = np.empty((g, 128, n, 4), np.uint8)
        nib[..., 0::2] = words & 0xF
        nib[..., 1::2] = words >> 4
        vals = E2M1[nib]
    vals = vals * np.repeat(np.exp2(scales.astype(np.float64) - 127.0), 8, axis=1)[..., None]
    return vals.transpose(0, 1, 3, 2).reshape(g * 512, n)


def gelu(v):
    return 0.5 * v * (1.0 + np.tanh(np.sqrt(2.0 / np.pi) * (v + 0.044715 * v**3)))


K, T, S, H, T2, N = 512, 2048, 1024, 1024, 2048, 384

def setup_inputs():
    n = np.random.standard_normal
    s = mx_kscale(K)[:, None]
    u = mx_kscale(H)[:, None]
    tab_words, tab_scales = pack_weight(n((K, T)) * s, "e4m3")
    wb_words, wb_scales = pack_weight(n((K, H)) / np.sqrt(K) / s * u.T, "e2m1")
    wa = (n((K, H)) / np.sqrt(K) / s).astype(np.float32)
    wo_words, wo_scales = pack_weight(n((H, N)) / np.sqrt(H) / u, "e4m3")
    return {
        "tab_words": tab_words, "tab_scales": tab_scales,
        "offs": striped(np.random.permutation(T)[:S]),
        "offs2": striped(np.random.permutation(T2)[:S]),
        "offs3": striped(np.random.permutation(T2)[:S]),
        "wb_words": wb_words, "wb_scales": wb_scales,
        "wa": wa,
        "wo_words": wo_words, "wo_scales": wo_scales,
        "wg1": np.exp(0.3 * n((128, S))).astype(np.float32),
        "wg2": np.exp(0.3 * n((128, S))).astype(np.float32),
        "res": (n((H, T2)) * u).astype(np.float32),
    }

def reference(tab_words, tab_scales, offs, offs2, offs3, wb_words, wb_scales, wa, wo_words, wo_scales, wg1, wg2, res):
    v = unpack_weight(tab_words, tab_scales, "e4m3")[:, unstriped(offs)]
    wb = unpack_weight(wb_words, wb_scales, "e2m1")
    wo = unpack_weight(wo_words, wo_scales, "e4m3")
    h1 = wb.T @ v
    h2 = mxq(f64(wa), 0, "e4m3").T @ v
    pageA = np.zeros((H, T2))
    pageA[:, unstriped(offs2)] = np.tile(f64(wg1), (H // 128, 1)) * h1
    pageB = np.zeros((H, T2))
    pageB[:, unstriped(offs3)] = np.tile(f64(wg2), (H // 128, 1)) * h2
    z = (pageA + f64(res)) / (1.0 + np.square(pageB))
    return wo.T @ mxq(z, 0, "e4m3")

@@ -1,0 +1,285 @@
+import math
+from contextlib import ExitStack
+
+import concourse.mybir as mybir
+from concourse.masks import make_identity
+
+K, T, S, H, T2, N = 512, 2048, 1024, 1024, 2048, 384
+FLOPS = 2 * K * H * S * 2 + 2 * H * N * T2
+
+F32 = mybir.dt.float32
+BF16 = mybir.dt.bfloat16
+I32 = mybir.dt.int32
+U32 = mybir.dt.uint32
+U16 = mybir.dt.uint16
+U8 = mybir.dt.uint8
+FP8X4 = mybir.dt.float8_e4m3fn_x4
+FP4X4 = mybir.dt.float4_e2m1fn_x4
+MULT = mybir.AluOpType.mult
+ACT = mybir.ActivationFunctionType
+
+P = 128
+PACK = 4
+BANK = 512
+TILES = H // P
+PASSES = H // (P * PACK)
+TILES_PER_PASS = TILES // PASSES
+CHUNKS = T2 // BANK
+BLOCKS = BANK // P
+HALVES = S // BANK
+WA_PARTS = ((0, 256), (256, 256), (512, 512))
+CENTRE = 1.375
+LIST_COLS = S // 16
+
+
+def tile_list_quota_bid_quotient_kernel(
+    tc, tab_words, tab_scales, offs, offs2, offs3, wb_words, wb_scales, wa, wo_words, wo_scales, wg1, wg2, res, out
+):
+    nc = tc.nc
+    with ExitStack() as ctx:
+        keep = ctx.enter_context(tc.tile_pool(name="keep", bufs=1))
+        ring = ctx.enter_context(tc.tile_pool(name="ring", bufs=2))
+        psum = ctx.enter_context(tc.psum_pool(name="psum", bufs=2))
+
+        pick = keep.tile([P, LIST_COLS], U16, name="pick")
+        bid_lots = keep.tile([P, LIST_COLS], U16, name="bid_lots")
+        ask_lots = keep.tile([P, LIST_COLS], U16, name="ask_lots")
+        tab_w = keep.tile([P, T], U32, name="tab_w", align_bytes=64)
+        tab_s = keep.tile([P, T], U8, name="tab_s", align_bytes=64)
+        wb_w = keep.tile([P, 2 * H], U8, name="wb_w", align_bytes=64)
+        wb_s = keep.tile([P, H], U8, name="wb_s", align_bytes=64)
+        wo_w = keep.tile([P, PASSES, N], U32, name="wo_w", align_bytes=64)
+        wo_s = keep.tile([P, PASSES, N], U8, name="wo_s", align_bytes=64)
+        gain = [keep.tile([P, S], F32, name=f"gain{i}") for i in range(2)]
+        ident = keep.tile([P, P], F32, name="ident")
+        pages = [keep.tile([P, T2], F32, name=f"page{i}") for i in range(2)]
+        landed = keep.tile([P, T // 4], I32, name="landed")
+
+        nc.sync.dma_start(pick[:], offs)
+        for q in range(4):
+            nc.sync.dma_start(landed[32 * q : 32 * q + 4, :], tab_scales[0, 4 * q : 4 * q + 4, :].bitcast(I32))
+        first_wa = keep.tile([P, PACK, 2 * P], F32, name="wa_raw0")
+        nc.sync.dma_start(first_wa[:], wa[:, 0 : 2 * P].rearrange("(p j) c -> p j c", j=PACK))
+        nc.sync.dma_start(tab_w[:].bitcast(I32), tab_words[0].rearrange("p t i -> p (t i)").bitcast(I32))
+        nc.vector.memset(tab_s[:].bitcast(I32), 0)
+        nc.vector.memset(pages[1][:], 0.0)
+        for q in range(4):
+            nc.vector.tensor_copy(tab_s[32 * q : 32 * q + 4, :].bitcast(I32), landed[32 * q : 32 * q + 4, :])
+        nc.gpsimd.memset(wb_s[:].bitcast(I32), 0)
+        nc.gpsimd.memset(wo_s[:].rearrange("p a n -> p (a n)").bitcast(I32), 0)
+        make_identity(nc, ident[:])
+        nc.gpsimd.memset(pages[0][:], 0.0)
+
+        halves = [slice(i * LIST_COLS // HALVES, (i + 1) * LIST_COLS // HALVES) for i in range(HALVES)]
+        v_w = [keep.tile([P, BANK], U32, name=f"v_w{i}", align_bytes=64) for i in range(HALVES)]
+        v_s = [keep.tile([P, BANK], U8, name=f"v_s{i}", align_bytes=64) for i in range(HALVES)]
+
+        def gather(into, table):
+            for i in range(HALVES):
+                nc.vector.tensor_copy(into[i][:], table[:].indirect(pick[:, halves[i]]))
+
+        wa_q = {}
+
+        def load_wa(c0, width):
+            raw = keep.tile([P, PACK, width], F32, name=f"wa_raw{c0}")
+            nc.sync.dma_start(raw[:], wa[:, c0 : c0 + width].rearrange("(p j) c -> p j c", j=PACK))
+            return raw
+
+        def quantise_wa(c0, width, raw):
+            woven = keep.tile([P, width, PACK], BF16, name=f"wa_woven{c0}", align_bytes=64)
+            nc.scalar.copy(woven[:], raw[:].rearrange("p j c -> p c j"))
+            codes = keep.tile([P, width], U32, name=f"wa_w{c0}", align_bytes=64)
+            scales = keep.tile([P, width], U8, name=f"wa_s{c0}", align_bytes=64)
+            nc.vector.quantize_mx(
+                out=codes[:].bitcast(FP8X4), scales=scales[:], in_=woven[:].rearrange("p c j -> p (c j)")
+            )
+            for c in range(0, width, P):
+                wa_q[(c0 + c) // P] = (codes[:, c : c + P].bitcast(FP8X4), scales[:, c : c + P])
+
+        feats = {}
+
+        def features(side, k):
+            if side == 0:
+                w = wb_w[:, 2 * P * k : 2 * P * (k + 1)].bitcast(FP4X4)
+                s = wb_s[:, P * k : P * (k + 1)]
+            else:
+                w, s = wa_q[k]
+            h = ring.tile([P, S], F32, name=f"h{side}")
+            for half in range(HALVES):
+                acc = psum.tile([P, BANK], F32, name="h_acc", tag="h_acc")
+                nc.tensor.matmul_mx(
+                    out=acc[:], lhsT=w, lhsT_scale=s, rhs=v_w[half][:].bitcast(FP8X4), rhs_scale=v_s[half][:],
+                    start=True, stop=True,
+                )
+                nc.scalar.copy(h[:, half * BANK : (half + 1) * BANK], acc[:])
+            feats[side, k] = h
+
+        def scatter(side, k, pieces=1):
+            lots = (bid_lots, ask_lots)[side]
+            page = pages[side]
+            for i in range(pieces):
+                entries = slice(i * S // pieces, (i + 1) * S // pieces)
+                cols = slice(i * LIST_COLS // pieces, (i + 1) * LIST_COLS // pieces)
+                nc.vector.tensor_tensor(
+                    page[:].indirect(lots[:, cols]), feats[side, k][:, entries], gain[side][:, entries], MULT
+                )
+
+        damp = {}
+
+        def squares(k):
+            page = pages[1]
+            d = ring.tile([P, T2], F32, name="damp")
+            for c in range(CHUNKS):
+                bank = psum.tile([P, BANK], F32, name="turned", tag="turned")
+                for b in range(BLOCKS):
+                    m0 = c * BANK + b * P
+                    nc.tensor.transpose(bank[:, b * P : (b + 1) * P], page[:, m0 : m0 + P], ident[:])
+                nc.scalar.activation(
+                    d[:, c * BANK : (c + 1) * BANK].rearrange("p (u b q e) -> p u b q e", u=2, b=BLOCKS, e=2),
+                    bank[:].rearrange("p (b q u e) -> p u b q e", b=BLOCKS, u=2, e=2),
+                    ACT.Square,
+                )
+            damp[k] = d
+
+        def damping(k):
+            d = damp[k]
+            for i in range(2):
+                part = d[:, i * T2 // 2 : (i + 1) * T2 // 2]
+                nc.scalar.activation(part, part, ACT.Abs_reciprocal_sqrt, bias=CENTRE, scale=CENTRE)
+            for i in range(2):
+                part = d[:, i * T2 // 2 : (i + 1) * T2 // 2]
+                nc.scalar.activation(part, part, ACT.Square, scale=math.sqrt(CENTRE))
+
+        sums = {}
+
+        def reserve(k):
+            rows = ring.tile([P, T2], F32, name="res_rows", bufs=3)
+            nc.sync.dma_start(rows[:], res[k * P : (k + 1) * P, :])
+            banks = []
+            for c in range(CHUNKS):
+                bank = psum.tile([P, BANK], F32, name="sum", tag="sum", bufs=4)
+                for b in range(BLOCKS):
+                    m0 = c * BANK + b * P
+                    nc.tensor.matmul(
+                        bank[:, b * P : (b + 1) * P], rows[:, m0 : m0 + P], ident[:],
+                        start=(b == 0), stop=False, is_transpose=True,
+                    )
+                banks.append(bank)
+            sums[k] = banks
+
+        z_t = {}
+
+        def quotient(k):
+            a, i = divmod(k, TILES_PER_PASS)
+            page = pages[0]
+            for c in range(CHUNKS):
+                bank = sums[k][c]
+                for b in range(BLOCKS):
+                    m0 = c * BANK + b * P
+                    nc.tensor.matmul(
+                        bank[:, b * P : (b + 1) * P], page[:, m0 : m0 + P], ident[:],
+                        start=False, stop=(b == BLOCKS - 1), is_transpose=True,
+                    )
+                if i == 0:
+                    z_t[a, c] = keep.tile([P, BLOCKS * BANK], BF16, name=f"z_t{a}_{c}")
+                place = z_t[a, c][:].rearrange("p (b u q e) -> p u b q e", b=BLOCKS, u=2, e=2)
+                nc.vector.tensor_tensor(
+                    place[:, :, :, 32 * i : 32 * (i + 1), :],
+                    bank[:].rearrange("p (b q u e) -> p u b q e", b=BLOCKS, u=2, e=2),
+                    damp[k][:, c * BANK : (c + 1) * BANK].rearrange("p (u b q e) -> p u b q e", u=2, b=BLOCKS, e=2),
+                    MULT,
+                )
+
+        z_q = {}
+
+        def quantise_z(a, c, tags, movers):
+            pairs = z_t[a, c][:].bitcast(F32)
+            woven = ring.tile([P, BANK * PACK], BF16, name="z_woven", align_bytes=64)
+            for j in range(2):
+                bank = psum.tile([P, BANK], F32, name="back", tag=tags[j])
+                for i in range(4):
+                    w0 = (4 * j + i) * P
+                    nc.tensor.transpose(bank[:, i * P : (i + 1) * P], pairs[:, w0 : w0 + P], ident[:])
+                movers[j](
+                    woven[:].bitcast(F32)[:, j * BANK : (j + 1) * BANK].rearrange("p (b m u) -> p b m u", b=2, u=2),
+                    bank[:].rearrange("p (b u m) -> p b m u", b=2, u=2),
+                )
+            codes = keep.tile([P, BANK], U32, name=f"z_w{a}_{c}", align_bytes=64)
+            scales = keep.tile([P, BANK], U8, name=f"z_s{a}_{c}", align_bytes=64)
+            nc.vector.quantize_mx(out=codes[:].bitcast(FP8X4), scales=scales[:], in_=woven[:])
+            z_q[a, c] = (codes, scales)
+
+        accs = {}
+
+        def score_pass(c, n, a, tag):
+            if a == 0:
+                accs[c, n] = psum.tile([P, BANK], F32, name="score", tag=tag, bufs=4 if tag == "sum" else 2)
+            nc.tensor.matmul_mx(
+                out=accs[c, n][:],
+                lhsT=wo_w[:, a, n * P : (n + 1) * P].bitcast(FP8X4),
+                lhsT_scale=wo_s[:, a, n * P : (n + 1) * P],
+                rhs=z_q[a, c][0][:].bitcast(FP8X4),
+                rhs_scale=z_q[a, c][1][:],
+                start=(a == 0),
+                stop=(a == PASSES - 1),
+            )
+
+        def scores(c, movers):
+            for n in range(N // P):
+                if (c, n) not in accs:
+                    score_pass(c, n, 0, "sum" if n else "h_acc")
+            for n in range(N // P):
+                score_pass(c, n, 1, None)
+                done = ring.tile([P, BANK], F32, name="done", bufs=6)
+                movers[n](done[:], accs[c, n][:])
+                nc.sync.dma_start(out[n * P : (n + 1) * P, c * BANK : (c + 1) * BANK], done[:])
+
+        act, dve = nc.scalar.copy, nc.vector.tensor_copy
+        nc.sync.dma_start(wb_w[:].bitcast(I32), wb_words[0].bitcast(I32))
+        for q in range(4):
+            nc.sync.dma_start(wb_s[32 * q : 32 * q + 4, :].bitcast(I32), wb_scales[0, 4 * q : 4 * q + 4, :].bitcast(I32))
+        nc.sync.dma_start(ask_lots[:], offs3)
+        nc.sync.dma_start(gain[1][:], wg2)
+        nc.sync.dma_start(bid_lots[:], offs2)
+        nc.sync.dma_start(gain[0][:], wg1)
+        gather(v_s, tab_s)
+        quantise_wa(*WA_PARTS[0], first_wa)
+        gather(v_w, tab_w)
+        features(1, 0)
+        scatter(1, 0, pieces=HALVES)
+        features(0, 0)
+        for k in range(TILES):
+            last = k + 1 == TILES
+            if not last:
+                features(1, k + 1)
+            scatter(0, k)
+            squares(k)
+            damping(k)
+            if not last:
+                scatter(1, k + 1)
+            reserve(k)
+            if k == 0:
+                for part in WA_PARTS[1:]:
+                    quantise_wa(*part, load_wa(*part))
+                nc.sync.dma_start(wo_w[:].bitcast(I32), wo_words.rearrange("a p n i -> p a (n i)").bitcast(I32))
+                for q in range(4):
+                    nc.sync.dma_start(
+                        wo_s[32 * q : 32 * q + 4, :, :].bitcast(I32),
+                        wo_scales[:, 4 * q : 4 * q + 4, :].rearrange("a r n -> r a n").bitcast(I32),
+                    )
+            if not last:
+                features(0, k + 1)
+            if k >= TILES_PER_PASS:
+                quantise_z(0, k - TILES_PER_PASS, ("turned", "turned"), (act, act))
+            if last:
+                for n in range(2):
+                    score_pass(0, n, 0, "h_acc")
+            quotient(k)
+        quantise_z(1, 0, ("turned", "turned"), (act, act))
+        quantise_z(1, 1, ("turned", "turned"), (act, dve))
+        scores(0, (act, dve, act))
+        quantise_z(1, 2, ("turned", "turned"), (act, dve))
+        scores(1, (act, dve, act))
+        quantise_z(1, 3, ("turned", "turned"), (act, dve))
+        scores(2, (act, act, act))
+        scores(3, (act, dve, act))

@@ -39,18 +39,20 @@ def tile_list_quota_bid_quotient_kernel(
     with ExitStack() as ctx:
         keep = ctx.enter_context(tc.tile_pool(name="keep", bufs=1))
         ring = ctx.enter_context(tc.tile_pool(name="ring", bufs=2))
+        reuse = ctx.enter_context(tc.tile_pool(name="reuse", bufs=1))
         psum = ctx.enter_context(tc.psum_pool(name="psum", bufs=2))
 
         pick = keep.tile([P, LIST_COLS], U16, name="pick")
         bid_lots = keep.tile([P, LIST_COLS], U16, name="bid_lots")
         ask_lots = keep.tile([P, LIST_COLS], U16, name="ask_lots")
-        tab_w = keep.tile([P, T], U32, name="tab_w", align_bytes=64)
+        tab_w = reuse.tile([P, T], U32, name="tab_w", offset=8 * S, align_bytes=64)
         tab_s = keep.tile([P, T], U8, name="tab_s", align_bytes=64)
         wb_w = keep.tile([P, 2 * H], U8, name="wb_w", align_bytes=64)
-        wb_s = keep.tile([P, H], U8, name="wb_s", align_bytes=64)
+        w_s = keep.tile([P, H + PASSES * N], U8, name="w_s", align_bytes=64)
+        wb_s = w_s[:, 0:H]
         wo_w = keep.tile([P, PASSES, N], U32, name="wo_w", align_bytes=64)
-        wo_s = keep.tile([P, PASSES, N], U8, name="wo_s", align_bytes=64)
-        gain = [keep.tile([P, S], F32, name=f"gain{i}") for i in range(2)]
+        wo_s = w_s[:, H:].rearrange("p (a n) -> p a n", a=PASSES)
+        gain = [reuse.tile([P, S], F32, name=f"gain{i}", offset=4 * S * (1 - i), align_bytes=64) for i in range(2)]
         ident = keep.tile([P, P], F32, name="ident")
         pages = [keep.tile([P, T2], F32, name=f"page{i}") for i in range(2)]
         landed = keep.tile([P, T // 4], I32, name="landed")
@@ -62,13 +64,12 @@ def tile_list_quota_bid_quotient_kernel(
         nc.sync.dma_start(first_wa[:], wa[:, 0 : 2 * P].rearrange("(p j) c -> p j c", j=PACK))
         nc.sync.dma_start(tab_w[:].bitcast(I32), tab_words[0].rearrange("p t i -> p (t i)").bitcast(I32))
         nc.vector.memset(tab_s[:].bitcast(I32), 0)
+        nc.vector.memset(w_s[:].bitcast(I32), 0)
         nc.vector.memset(pages[1][:], 0.0)
         for q in range(4):
             nc.vector.tensor_copy(tab_s[32 * q : 32 * q + 4, :].bitcast(I32), landed[32 * q : 32 * q + 4, :])
-        nc.gpsimd.memset(wb_s[:].bitcast(I32), 0)
-        nc.gpsimd.memset(wo_s[:].rearrange("p a n -> p (a n)").bitcast(I32), 0)
         make_identity(nc, ident[:])
-        nc.gpsimd.memset(pages[0][:], 0.0)
+        nc.vector.memset(pages[0][:], 0.0)
 
         halves = [slice(i * LIST_COLS // HALVES, (i + 1) * LIST_COLS // HALVES) for i in range(HALVES)]
         v_w = [keep.tile([P, BANK], U32, name=f"v_w{i}", align_bytes=64) for i in range(HALVES)]
@@ -104,30 +105,39 @@ def tile_list_quota_bid_quotient_kernel(
                 s = wb_s[:, P * k : P * (k + 1)]
             else:
                 w, s = wa_q[k]
-            h = ring.tile([P, S], F32, name=f"h{side}")
+            h = ring.tile([P, S], F32, name=f"h{side}", tag=f"h{side}", align_bytes=64)
             for half in range(HALVES):
                 acc = psum.tile([P, BANK], F32, name="h_acc", tag="h_acc")
                 nc.tensor.matmul_mx(
                     out=acc[:], lhsT=w, lhsT_scale=s, rhs=v_w[half][:].bitcast(FP8X4), rhs_scale=v_s[half][:],
                     start=True, stop=True,
                 )
-                nc.scalar.copy(h[:, half * BANK : (half + 1) * BANK], acc[:])
+                part = slice(half * BANK, (half + 1) * BANK)
+                if (side, k) == (1, 0):
+                    nc.vector.tensor_tensor(h[:, part], acc[:], gain[side][:, part], MULT)
+                    continue
+                nc.scalar.copy(h[:, part], acc[:])
+                if k > 0:
+                    nc.gpsimd.tensor_tensor(h[:, part], h[:, part], gain[side][:, part], MULT)
             feats[side, k] = h
 
         def scatter(side, k, pieces=1):
             lots = (bid_lots, ask_lots)[side]
-            page = pages[side]
+            page = pages[side + side * (k % 2)]
             for i in range(pieces):
                 entries = slice(i * S // pieces, (i + 1) * S // pieces)
                 cols = slice(i * LIST_COLS // pieces, (i + 1) * LIST_COLS // pieces)
-                nc.vector.tensor_tensor(
-                    page[:].indirect(lots[:, cols]), feats[side, k][:, entries], gain[side][:, entries], MULT
-                )
+                if (side, k) == (0, 0):
+                    nc.vector.tensor_tensor(
+                        page[:].indirect(lots[:, cols]), feats[side, k][:, entries], gain[side][:, entries], MULT
+                    )
+                else:
+                    nc.vector.tensor_copy(page[:].indirect(lots[:, cols]), feats[side, k][:, entries])
 
         damp = {}
 
         def squares(k):
-            page = pages[1]
+            page = pages[1 + k % 2]
             d = ring.tile([P, T2], F32, name="damp")
             for c in range(CHUNKS):
                 bank = psum.tile([P, BANK], F32, name="turned", tag="turned")
@@ -146,8 +156,6 @@ def tile_list_quota_bid_quotient_kernel(
             for i in range(2):
                 part = d[:, i * T2 // 2 : (i + 1) * T2 // 2]
                 nc.scalar.activation(part, part, ACT.Abs_reciprocal_sqrt, bias=CENTRE, scale=CENTRE)
-            for i in range(2):
-                part = d[:, i * T2 // 2 : (i + 1) * T2 // 2]
                 nc.scalar.activation(part, part, ACT.Square, scale=math.sqrt(CENTRE))
 
         sums = {}
@@ -183,18 +191,26 @@ def tile_list_quota_bid_quotient_kernel(
                 if i == 0:
                     z_t[a, c] = keep.tile([P, BLOCKS * BANK], BF16, name=f"z_t{a}_{c}")
                 place = z_t[a, c][:].rearrange("p (b u q e) -> p u b q e", b=BLOCKS, u=2, e=2)
-                nc.vector.tensor_tensor(
+                total = bank[:].rearrange("p (b q u e) -> p u b q e", b=BLOCKS, u=2, e=2)
+                engine = nc.vector
+                if k + 1 < TILES:
+                    held = ring.tile([P, BANK], F32, name="held", bufs=4)
+                    ordered = held[:].rearrange("p (u b q e) -> p u b q e", u=2, b=BLOCKS, e=2)
+                    nc.scalar.copy(ordered, total)
+                    total, engine = ordered, nc.gpsimd
+                engine.tensor_tensor(
                     place[:, :, :, 32 * i : 32 * (i + 1), :],
-                    bank[:].rearrange("p (b q u e) -> p u b q e", b=BLOCKS, u=2, e=2),
+                    total,
                     damp[k][:, c * BANK : (c + 1) * BANK].rearrange("p (u b q e) -> p u b q e", u=2, b=BLOCKS, e=2),
                     MULT,
                 )
 
         z_q = {}
+        z_woven = {}
 
-        def quantise_z(a, c, tags, movers):
+        def weave_z(a, c, tags, movers):
             pairs = z_t[a, c][:].bitcast(F32)
-            woven = ring.tile([P, BANK * PACK], BF16, name="z_woven", align_bytes=64)
+            woven = ring.tile([P, BANK * PACK], BF16, name="z_woven", bufs=4, align_bytes=64)
             for j in range(2):
                 bank = psum.tile([P, BANK], F32, name="back", tag=tags[j])
                 for i in range(4):
@@ -204,7 +220,14 @@ def tile_list_quota_bid_quotient_kernel(
                     woven[:].bitcast(F32)[:, j * BANK : (j + 1) * BANK].rearrange("p (b m u) -> p b m u", b=2, u=2),
                     bank[:].rearrange("p (b u m) -> p b m u", b=2, u=2),
                 )
-            codes = keep.tile([P, BANK], U32, name=f"z_w{a}_{c}", align_bytes=64)
+            z_woven[a, c] = woven
+
+        def quantise_z(a, c):
+            woven = z_woven[a, c]
+            if a == 0:
+                codes = reuse.tile([P, BANK], U32, name=f"z_w0_{c}", offset=4 * BANK * c, align_bytes=64)
+            else:
+                codes = keep.tile([P, BANK], U32, name=f"z_w{a}_{c}", align_bytes=64)
             scales = keep.tile([P, BANK], U8, name=f"z_s{a}_{c}", align_bytes=64)
             nc.vector.quantize_mx(out=codes[:].bitcast(FP8X4), scales=scales[:], in_=woven[:])
             z_q[a, c] = (codes, scales)
@@ -245,15 +268,21 @@ def tile_list_quota_bid_quotient_kernel(
         gather(v_s, tab_s)
         quantise_wa(*WA_PARTS[0], first_wa)
         gather(v_w, tab_w)
+        pages.append(reuse.tile([P, T2], F32, name="page2", offset=8 * S, align_bytes=64))
+        nc.gpsimd.memset(pages[2][:], 0.0)
         features(1, 0)
         scatter(1, 0, pieces=HALVES)
+        features(1, 1)
         features(0, 0)
         for k in range(TILES):
             last = k + 1 == TILES
-            if not last:
-                features(1, k + 1)
+            if last:
+                for c in range(CHUNKS):
+                    quantise_z(0, c)
             scatter(0, k)
             squares(k)
+            if not last:
+                features(0, k + 1)
             damping(k)
             if not last:
                 scatter(1, k + 1)
@@ -267,19 +296,23 @@ def tile_list_quota_bid_quotient_kernel(
                         wo_s[32 * q : 32 * q + 4, :, :].bitcast(I32),
                         wo_scales[:, 4 * q : 4 * q + 4, :].rearrange("a r n -> r a n").bitcast(I32),
                     )
-            if not last:
-                features(0, k + 1)
-            if k >= TILES_PER_PASS:
-                quantise_z(0, k - TILES_PER_PASS, ("turned", "turned"), (act, act))
+            for c in {4: [0], 5: [1], 6: [2, 3]}.get(k, []):
+                weave_z(0, c, ("turned", "turned"), (act, act))
             if last:
                 for n in range(2):
                     score_pass(0, n, 0, "h_acc")
+            if k + 2 < TILES:
+                features(1, k + 2)
             quotient(k)
-        quantise_z(1, 0, ("turned", "turned"), (act, act))
-        quantise_z(1, 1, ("turned", "turned"), (act, dve))
+        weave_z(1, 0, ("turned", "turned"), (act, act))
+        quantise_z(1, 0)
+        weave_z(1, 1, ("turned", "turned"), (act, dve))
+        quantise_z(1, 1)
         scores(0, (act, dve, act))
-        quantise_z(1, 2, ("turned", "turned"), (act, dve))
+        weave_z(1, 2, ("turned", "turned"), (act, dve))
+        quantise_z(1, 2)
         scores(1, (act, dve, act))
-        quantise_z(1, 3, ("turned", "turned"), (act, dve))
+        weave_z(1, 3, ("turned", "turned"), (act, dve))
+        quantise_z(1, 3)
         scores(2, (act, act, act))
         scores(3, (act, dve, act))

@@ -27,7 +27,8 @@ TILES_PER_PASS = TILES // PASSES
 CHUNKS = T2 // BANK
 BLOCKS = BANK // P
 HALVES = S // BANK
-WA_PARTS = ((0, 256), (256, 256), (512, 512))
+WA_HALF = 512
+WA_FIRST = ((0, 128), (128, 128), (256, 256))
 CENTRE = 1.375
 LIST_COLS = S // 16
 
@@ -46,30 +47,28 @@ def tile_list_quota_bid_quotient_kernel(
         bid_lots = keep.tile([P, LIST_COLS], U16, name="bid_lots")
         ask_lots = keep.tile([P, LIST_COLS], U16, name="ask_lots")
         tab_w = reuse.tile([P, T], U32, name="tab_w", offset=8 * S, align_bytes=64)
-        tab_s = keep.tile([P, T], U8, name="tab_s", align_bytes=64)
+        tab_s = reuse.tile([P, T], U8, name="tab_s", offset=17 * S, align_bytes=64)
         wb_w = keep.tile([P, 2 * H], U8, name="wb_w", align_bytes=64)
         w_s = keep.tile([P, H + PASSES * N], U8, name="w_s", align_bytes=64)
         wb_s = w_s[:, 0:H]
         wo_w = keep.tile([P, PASSES, N], U32, name="wo_w", align_bytes=64)
         wo_s = w_s[:, H:].rearrange("p (a n) -> p a n", a=PASSES)
-        gain = [reuse.tile([P, S], F32, name=f"gain{i}", offset=4 * S * (1 - i), align_bytes=64) for i in range(2)]
+        gain = [reuse.tile([P, S], F32, name=f"gain{i}", offset=4 * S * i, align_bytes=64) for i in range(2)]
         ident = keep.tile([P, P], F32, name="ident")
-        pages = [keep.tile([P, T2], F32, name=f"page{i}") for i in range(2)]
-        landed = keep.tile([P, T // 4], I32, name="landed")
+        pages = {(1, 0): keep.tile([P, T2], F32, name="page10")}
 
+        nc.vector.memset(tab_s[:].bitcast(I32), 0)
         nc.sync.dma_start(pick[:], offs)
         for q in range(4):
-            nc.sync.dma_start(landed[32 * q : 32 * q + 4, :], tab_scales[0, 4 * q : 4 * q + 4, :].bitcast(I32))
-        first_wa = keep.tile([P, PACK, 2 * P], F32, name="wa_raw0")
-        nc.sync.dma_start(first_wa[:], wa[:, 0 : 2 * P].rearrange("(p j) c -> p j c", j=PACK))
+            nc.sync.dma_start(tab_s[32 * q : 32 * q + 4, :].bitcast(I32), tab_scales[0, 4 * q : 4 * q + 4, :].bitcast(I32))
         nc.sync.dma_start(tab_w[:].bitcast(I32), tab_words[0].rearrange("p t i -> p (t i)").bitcast(I32))
-        nc.vector.memset(tab_s[:].bitcast(I32), 0)
+        first_wa = reuse.tile([P, PACK, WA_HALF], F32, name="wa_raw0", offset=24 * S, align_bytes=64)
+        nc.sync.dma_start(first_wa[:], wa[:, 0:WA_HALF].rearrange("(p j) c -> p j c", j=PACK))
         nc.vector.memset(w_s[:].bitcast(I32), 0)
-        nc.vector.memset(pages[1][:], 0.0)
-        for q in range(4):
-            nc.vector.tensor_copy(tab_s[32 * q : 32 * q + 4, :].bitcast(I32), landed[32 * q : 32 * q + 4, :])
+        nc.vector.memset(pages[1, 0][:], 0.0)
         make_identity(nc, ident[:])
-        nc.vector.memset(pages[0][:], 0.0)
+        pages[0, 0] = keep.tile([P, T2], F32, name="page00")
+        nc.vector.memset(pages[0, 0][:], 0.0)
 
         halves = [slice(i * LIST_COLS // HALVES, (i + 1) * LIST_COLS // HALVES) for i in range(HALVES)]
         v_w = [keep.tile([P, BANK], U32, name=f"v_w{i}", align_bytes=64) for i in range(HALVES)]
@@ -87,8 +86,12 @@ def tile_list_quota_bid_quotient_kernel(
             return raw
 
         def quantise_wa(c0, width, raw):
-            woven = keep.tile([P, width, PACK], BF16, name=f"wa_woven{c0}", align_bytes=64)
-            nc.scalar.copy(woven[:], raw[:].rearrange("p j c -> p c j"))
+            if c0 < WA_HALF:
+                at = {0: 19, 128: 20, 256: 15}[c0] * S
+                woven = reuse.tile([P, width, PACK], BF16, name=f"wa_woven{c0}", offset=at, align_bytes=64)
+            else:
+                woven = keep.tile([P, width, PACK], BF16, name=f"wa_woven{c0}", align_bytes=64)
+            nc.scalar.copy(woven[:], raw.rearrange("p j c -> p c j"))
             codes = keep.tile([P, width], U32, name=f"wa_w{c0}", align_bytes=64)
             scales = keep.tile([P, width], U8, name=f"wa_s{c0}", align_bytes=64)
             nc.vector.quantize_mx(
@@ -105,9 +108,9 @@ def tile_list_quota_bid_quotient_kernel(
                 s = wb_s[:, P * k : P * (k + 1)]
             else:
                 w, s = wa_q[k]
-            h = ring.tile([P, S], F32, name=f"h{side}", tag=f"h{side}", align_bytes=64)
+            h = reuse.tile([P, S], F32, name=f"h{side}_{k}", offset=(24 + 8 * side + 4 * (k % 2)) * S, align_bytes=64)
             for half in range(HALVES):
-                acc = psum.tile([P, BANK], F32, name="h_acc", tag="h_acc")
+                acc = psum.tile([P, BANK], F32, name="h_acc", tag="turned" if (side, k) == (1, 0) else "h_acc")
                 nc.tensor.matmul_mx(
                     out=acc[:], lhsT=w, lhsT_scale=s, rhs=v_w[half][:].bitcast(FP8X4), rhs_scale=v_s[half][:],
                     start=True, stop=True,
@@ -123,7 +126,7 @@ def tile_list_quota_bid_quotient_kernel(
 
         def scatter(side, k, pieces=1):
             lots = (bid_lots, ask_lots)[side]
-            page = pages[side + side * (k % 2)]
+            page = pages[side, k % 2]
             for i in range(pieces):
                 entries = slice(i * S // pieces, (i + 1) * S // pieces)
                 cols = slice(i * LIST_COLS // pieces, (i + 1) * LIST_COLS // pieces)
@@ -137,7 +140,7 @@ def tile_list_quota_bid_quotient_kernel(
         damp = {}
 
         def squares(k):
-            page = pages[1 + k % 2]
+            page = pages[1, k % 2]
             d = ring.tile([P, T2], F32, name="damp")
             for c in range(CHUNKS):
                 bank = psum.tile([P, BANK], F32, name="turned", tag="turned")
@@ -160,9 +163,16 @@ def tile_list_quota_bid_quotient_kernel(
 
         sums = {}
 
+        res_rows = {}
+
+        def load_res(k):
+            res_rows[k] = ring.tile([P, T2], F32, name="res_rows", bufs=3)
+            nc.sync.dma_start(res_rows[k][:], res[k * P : (k + 1) * P, :])
+
         def reserve(k):
-            rows = ring.tile([P, T2], F32, name="res_rows", bufs=3)
-            nc.sync.dma_start(rows[:], res[k * P : (k + 1) * P, :])
+            if k not in res_rows:
+                load_res(k)
+            rows = res_rows[k]
             banks = []
             for c in range(CHUNKS):
                 bank = psum.tile([P, BANK], F32, name="sum", tag="sum", bufs=4)
@@ -179,7 +189,7 @@ def tile_list_quota_bid_quotient_kernel(
 
         def quotient(k):
             a, i = divmod(k, TILES_PER_PASS)
-            page = pages[0]
+            page = pages[0, k % 2]
             for c in range(CHUNKS):
                 bank = sums[k][c]
                 for b in range(BLOCKS):
@@ -225,7 +235,7 @@ def tile_list_quota_bid_quotient_kernel(
         def quantise_z(a, c):
             woven = z_woven[a, c]
             if a == 0:
-                codes = reuse.tile([P, BANK], U32, name=f"z_w0_{c}", offset=4 * BANK * c, align_bytes=64)
+                codes = reuse.tile([P, BANK], U32, name=f"z_w0_{c}", offset=24 * S + 4 * BANK * c, align_bytes=64)
             else:
                 codes = keep.tile([P, BANK], U32, name=f"z_w{a}_{c}", align_bytes=64)
             scales = keep.tile([P, BANK], U8, name=f"z_s{a}_{c}", align_bytes=64)
@@ -265,21 +275,28 @@ def tile_list_quota_bid_quotient_kernel(
         nc.sync.dma_start(gain[1][:], wg2)
         nc.sync.dma_start(bid_lots[:], offs2)
         nc.sync.dma_start(gain[0][:], wg1)
+        load_res(0)
         gather(v_s, tab_s)
-        quantise_wa(*WA_PARTS[0], first_wa)
         gather(v_w, tab_w)
-        pages.append(reuse.tile([P, T2], F32, name="page2", offset=8 * S, align_bytes=64))
-        nc.gpsimd.memset(pages[2][:], 0.0)
+        for c0, width in WA_FIRST:
+            quantise_wa(c0, width, first_wa[:, :, c0 : c0 + width])
+        pages[1, 1] = reuse.tile([P, T2], F32, name="page11", offset=16 * S, align_bytes=64)
+        pages[0, 1] = reuse.tile([P, T2], F32, name="page01", offset=8 * S, align_bytes=64)
+        nc.gpsimd.memset(pages[1, 1][:], 0.0)
         features(1, 0)
         scatter(1, 0, pieces=HALVES)
         features(1, 1)
         features(0, 0)
+        nc.gpsimd.memset(pages[0, 1][:], 0.0)
         for k in range(TILES):
             last = k + 1 == TILES
-            if last:
-                for c in range(CHUNKS):
-                    quantise_z(0, c)
             scatter(0, k)
+            if k + 2 == TILES:
+                for c in (0, 1):
+                    quantise_z(0, c)
+            if last:
+                for c in (2, 3):
+                    quantise_z(0, c)
             squares(k)
             if not last:
                 features(0, k + 1)
@@ -288,15 +305,15 @@ def tile_list_quota_bid_quotient_kernel(
                 scatter(1, k + 1)
             reserve(k)
             if k == 0:
-                for part in WA_PARTS[1:]:
-                    quantise_wa(*part, load_wa(*part))
+                quantise_wa(WA_HALF, WA_HALF, load_wa(WA_HALF, WA_HALF)[:])
+            if k == 2:
                 nc.sync.dma_start(wo_w[:].bitcast(I32), wo_words.rearrange("a p n i -> p a (n i)").bitcast(I32))
                 for q in range(4):
                     nc.sync.dma_start(
                         wo_s[32 * q : 32 * q + 4, :, :].bitcast(I32),
                         wo_scales[:, 4 * q : 4 * q + 4, :].rearrange("a r n -> r a n").bitcast(I32),
                     )
-            for c in {4: [0], 5: [1], 6: [2, 3]}.get(k, []):
+            for c in {4: [0, 1], 5: [2], 6: [3]}.get(k, []):
                 weave_z(0, c, ("turned", "turned"), (act, act))
             if last:
                 for n in range(2):

@@ -154,12 +154,22 @@ def tile_list_quota_bid_quotient_kernel(
                 )
             damp[k] = d
 
+        def helped(k, c):
+            return 4 <= k < 7 and c >= CHUNKS - 2
+
         def damping(k):
             d = damp[k]
             for i in range(2):
                 part = d[:, i * T2 // 2 : (i + 1) * T2 // 2]
                 nc.scalar.activation(part, part, ACT.Abs_reciprocal_sqrt, bias=CENTRE, scale=CENTRE)
-                nc.scalar.activation(part, part, ACT.Square, scale=math.sqrt(CENTRE))
+                for c in (2 * i, 2 * i + 1):
+                    if helped(k, c):
+                        piece = d[:, c * BANK : (c + 1) * BANK]
+                        nc.gpsimd.tensor_tensor(piece, piece, piece, MULT)
+                own = [c for c in (2 * i, 2 * i + 1) if not helped(k, c)]
+                if own:
+                    piece = d[:, own[0] * BANK : (own[-1] + 1) * BANK]
+                    nc.scalar.activation(piece, piece, ACT.Square, scale=math.sqrt(CENTRE))
 
         sums = {}
 
@@ -206,7 +216,10 @@ def tile_list_quota_bid_quotient_kernel(
                 if k + 1 < TILES:
                     held = ring.tile([P, BANK], F32, name="held", bufs=4)
                     ordered = held[:].rearrange("p (u b q e) -> p u b q e", u=2, b=BLOCKS, e=2)
-                    nc.scalar.copy(ordered, total)
+                    if helped(k, c):
+                        nc.scalar.activation(ordered, total, ACT.Copy, scale=CENTRE)
+                    else:
+                        nc.scalar.copy(ordered, total)
                     total, engine = ordered, nc.gpsimd
                 engine.tensor_tensor(
                     place[:, :, :, 32 * i : 32 * (i + 1), :],
@@ -235,7 +248,7 @@ def tile_list_quota_bid_quotient_kernel(
         def quantise_z(a, c):
             woven = z_woven[a, c]
             if a == 0:
-                codes = reuse.tile([P, BANK], U32, name=f"z_w0_{c}", offset=24 * S + 4 * BANK * c, align_bytes=64)
+                codes = reuse.tile([P, BANK], U32, name=f"z_w0_{c}", offset=(28 if c < 2 else 4) * S + 4 * BANK * c, align_bytes=64)
             else:
                 codes = keep.tile([P, BANK], U32, name=f"z_w{a}_{c}", align_bytes=64)
             scales = keep.tile([P, BANK], U8, name=f"z_s{a}_{c}", align_bytes=64)
@@ -291,11 +304,8 @@ def tile_list_quota_bid_quotient_kernel(
         for k in range(TILES):
             last = k + 1 == TILES
             scatter(0, k)
-            if k + 2 == TILES:
-                for c in (0, 1):
-                    quantise_z(0, c)
             if last:
-                for c in (2, 3):
+                for c in (0, 1):
                     quantise_z(0, c)
             squares(k)
             if not last:
@@ -315,19 +325,20 @@ def tile_list_quota_bid_quotient_kernel(
                     )
             for c in {4: [0, 1], 5: [2], 6: [3]}.get(k, []):
                 weave_z(0, c, ("turned", "turned"), (act, act))
-            if last:
-                for n in range(2):
-                    score_pass(0, n, 0, "h_acc")
             if k + 2 < TILES:
                 features(1, k + 2)
             quotient(k)
+        for n in range(2):
+            score_pass(0, n, 0, "h_acc")
         weave_z(1, 0, ("turned", "turned"), (act, act))
         quantise_z(1, 0)
         weave_z(1, 1, ("turned", "turned"), (act, dve))
         quantise_z(1, 1)
+        quantise_z(0, 2)
         scores(0, (act, dve, act))
         weave_z(1, 2, ("turned", "turned"), (act, dve))
         quantise_z(1, 2)
+        quantise_z(0, 3)
         scores(1, (act, dve, act))
         weave_z(1, 3, ("turned", "turned"), (act, dve))
         quantise_z(1, 3)

@@ -143,7 +143,7 @@ def tile_list_quota_bid_quotient_kernel(
             page = pages[1, k % 2]
             d = ring.tile([P, T2], F32, name="damp")
             for c in range(CHUNKS):
-                bank = psum.tile([P, BANK], F32, name="turned", tag="turned")
+                bank = psum.tile([P, BANK], F32, name="turned", tag="h_acc" if k + 1 == TILES and c >= 2 else "turned")
                 for b in range(BLOCKS):
                     m0 = c * BANK + b * P
                     nc.tensor.transpose(bank[:, b * P : (b + 1) * P], page[:, m0 : m0 + P], ident[:])

import math
from contextlib import ExitStack

import concourse.mybir as mybir
from concourse.masks import make_identity

K, T, S, H, T2, N = 512, 2048, 1024, 1024, 2048, 384
FLOPS = 2 * K * H * S * 2 + 2 * H * N * T2

F32 = mybir.dt.float32
BF16 = mybir.dt.bfloat16
I32 = mybir.dt.int32
U32 = mybir.dt.uint32
U16 = mybir.dt.uint16
U8 = mybir.dt.uint8
FP8X4 = mybir.dt.float8_e4m3fn_x4
FP4X4 = mybir.dt.float4_e2m1fn_x4
MULT = mybir.AluOpType.mult
ACT = mybir.ActivationFunctionType

P = 128
PACK = 4
BANK = 512
TILES = H // P
PASSES = H // (P * PACK)
TILES_PER_PASS = TILES // PASSES
CHUNKS = T2 // BANK
BLOCKS = BANK // P
HALVES = S // BANK
WA_HALF = 512
WA_FIRST = ((0, 128), (128, 128), (256, 256))
CENTRE = 1.375
LIST_COLS = S // 16


def tile_list_quota_bid_quotient_kernel(
    tc, tab_words, tab_scales, offs, offs2, offs3, wb_words, wb_scales, wa, wo_words, wo_scales, wg1, wg2, res, out
):
    nc = tc.nc
    with ExitStack() as ctx:
        keep = ctx.enter_context(tc.tile_pool(name="keep", bufs=1))
        ring = ctx.enter_context(tc.tile_pool(name="ring", bufs=2))
        reuse = ctx.enter_context(tc.tile_pool(name="reuse", bufs=1))
        psum = ctx.enter_context(tc.psum_pool(name="psum", bufs=2))

        pick = keep.tile([P, LIST_COLS], U16, name="pick")
        bid_lots = keep.tile([P, LIST_COLS], U16, name="bid_lots")
        ask_lots = keep.tile([P, LIST_COLS], U16, name="ask_lots")
        tab_w = reuse.tile([P, T], U32, name="tab_w", offset=8 * S, align_bytes=64)
        tab_s = reuse.tile([P, T], U8, name="tab_s", offset=17 * S, align_bytes=64)
        wb_w = keep.tile([P, 2 * H], U8, name="wb_w", align_bytes=64)
        w_s = keep.tile([P, H + PASSES * N], U8, name="w_s", align_bytes=64)
        wb_s = w_s[:, 0:H]
        wo_w = keep.tile([P, PASSES, N], U32, name="wo_w", align_bytes=64)
        wo_s = w_s[:, H:].rearrange("p (a n) -> p a n", a=PASSES)
        gain = [reuse.tile([P, S], F32, name=f"gain{i}", offset=4 * S * i, align_bytes=64) for i in range(2)]
        ident = keep.tile([P, P], F32, name="ident")
        pages = {(1, 0): keep.tile([P, T2], F32, name="page10")}

        nc.vector.memset(tab_s[:].bitcast(I32), 0)
        nc.sync.dma_start(pick[:], offs)
        for q in range(4):
            nc.sync.dma_start(tab_s[32 * q : 32 * q + 4, :].bitcast(I32), tab_scales[0, 4 * q : 4 * q + 4, :].bitcast(I32))
        nc.sync.dma_start(tab_w[:].bitcast(I32), tab_words[0].rearrange("p t i -> p (t i)").bitcast(I32))
        first_wa = reuse.tile([P, PACK, WA_HALF], F32, name="wa_raw0", offset=24 * S, align_bytes=64)
        nc.sync.dma_start(first_wa[:], wa[:, 0:WA_HALF].rearrange("(p j) c -> p j c", j=PACK))
        nc.vector.memset(w_s[:].bitcast(I32), 0)
        nc.vector.memset(pages[1, 0][:], 0.0)
        make_identity(nc, ident[:])
        pages[0, 0] = keep.tile([P, T2], F32, name="page00")
        nc.vector.memset(pages[0, 0][:], 0.0)

        halves = [slice(i * LIST_COLS // HALVES, (i + 1) * LIST_COLS // HALVES) for i in range(HALVES)]
        v_w = [keep.tile([P, BANK], U32, name=f"v_w{i}", align_bytes=64) for i in range(HALVES)]
        v_s = [keep.tile([P, BANK], U8, name=f"v_s{i}", align_bytes=64) for i in range(HALVES)]

        def gather(into, table):
            for i in range(HALVES):
                nc.vector.tensor_copy(into[i][:], table[:].indirect(pick[:, halves[i]]))

        wa_q = {}

        def load_wa(c0, width):
            raw = keep.tile([P, PACK, width], F32, name=f"wa_raw{c0}")
            nc.sync.dma_start(raw[:], wa[:, c0 : c0 + width].rearrange("(p j) c -> p j c", j=PACK))
            return raw

        def quantise_wa(c0, width, raw):
            if c0 < WA_HALF:
                at = {0: 19, 128: 20, 256: 15}[c0] * S
                woven = reuse.tile([P, width, PACK], BF16, name=f"wa_woven{c0}", offset=at, align_bytes=64)
            else:
                woven = keep.tile([P, width, PACK], BF16, name=f"wa_woven{c0}", align_bytes=64)
            nc.scalar.copy(woven[:], raw.rearrange("p j c -> p c j"))
            codes = keep.tile([P, width], U32, name=f"wa_w{c0}", align_bytes=64)
            scales = keep.tile([P, width], U8, name=f"wa_s{c0}", align_bytes=64)
            nc.vector.quantize_mx(
                out=codes[:].bitcast(FP8X4), scales=scales[:], in_=woven[:].rearrange("p c j -> p (c j)")
            )
            for c in range(0, width, P):
                wa_q[(c0 + c) // P] = (codes[:, c : c + P].bitcast(FP8X4), scales[:, c : c + P])

        feats = {}

        def features(side, k):
            if side == 0:
                w = wb_w[:, 2 * P * k : 2 * P * (k + 1)].bitcast(FP4X4)
                s = wb_s[:, P * k : P * (k + 1)]
            else:
                w, s = wa_q[k]
            h = reuse.tile([P, S], F32, name=f"h{side}_{k}", offset=(24 + 8 * side + 4 * (k % 2)) * S, align_bytes=64)
            for half in range(HALVES):
                acc = psum.tile([P, BANK], F32, name="h_acc", tag="turned" if (side, k) == (1, 0) else "h_acc")
                nc.tensor.matmul_mx(
                    out=acc[:], lhsT=w, lhsT_scale=s, rhs=v_w[half][:].bitcast(FP8X4), rhs_scale=v_s[half][:],
                    start=True, stop=True,
                )
                part = slice(half * BANK, (half + 1) * BANK)
                if (side, k) == (1, 0):
                    nc.vector.tensor_tensor(h[:, part], acc[:], gain[side][:, part], MULT)
                    continue
                nc.scalar.copy(h[:, part], acc[:])
                if k > 0:
                    nc.gpsimd.tensor_tensor(h[:, part], h[:, part], gain[side][:, part], MULT)
            feats[side, k] = h

        def scatter(side, k, pieces=1):
            lots = (bid_lots, ask_lots)[side]
            page = pages[side, k % 2]
            for i in range(pieces):
                entries = slice(i * S // pieces, (i + 1) * S // pieces)
                cols = slice(i * LIST_COLS // pieces, (i + 1) * LIST_COLS // pieces)
                if (side, k) == (0, 0):
                    nc.vector.tensor_tensor(
                        page[:].indirect(lots[:, cols]), feats[side, k][:, entries], gain[side][:, entries], MULT
                    )
                else:
                    nc.vector.tensor_copy(page[:].indirect(lots[:, cols]), feats[side, k][:, entries])

        damp = {}

        def squares(k):
            page = pages[1, k % 2]
            d = ring.tile([P, T2], F32, name="damp")
            for c in range(CHUNKS):
                bank = psum.tile([P, BANK], F32, name="turned", tag="h_acc" if k + 1 == TILES and c >= 2 else "turned")
                for b in range(BLOCKS):
                    m0 = c * BANK + b * P
                    nc.tensor.transpose(bank[:, b * P : (b + 1) * P], page[:, m0 : m0 + P], ident[:])
                nc.scalar.activation(
                    d[:, c * BANK : (c + 1) * BANK].rearrange("p (u b q e) -> p u b q e", u=2, b=BLOCKS, e=2),
                    bank[:].rearrange("p (b q u e) -> p u b q e", b=BLOCKS, u=2, e=2),
                    ACT.Square,
                )
            damp[k] = d

        def helped(k, c):
            return 4 <= k < 7 and c >= CHUNKS - 2

        def damping(k):
            d = damp[k]
            for i in range(2):
                part = d[:, i * T2 // 2 : (i + 1) * T2 // 2]
                nc.scalar.activation(part, part, ACT.Abs_reciprocal_sqrt, bias=CENTRE, scale=CENTRE)
                for c in (2 * i, 2 * i + 1):
                    if helped(k, c):
                        piece = d[:, c * BANK : (c + 1) * BANK]
                        nc.gpsimd.tensor_tensor(piece, piece, piece, MULT)
                own = [c for c in (2 * i, 2 * i + 1) if not helped(k, c)]
                if own:
                    piece = d[:, own[0] * BANK : (own[-1] + 1) * BANK]
                    nc.scalar.activation(piece, piece, ACT.Square, scale=math.sqrt(CENTRE))

        sums = {}

        res_rows = {}

        def load_res(k):
            res_rows[k] = ring.tile([P, T2], F32, name="res_rows", bufs=3)
            nc.sync.dma_start(res_rows[k][:], res[k * P : (k + 1) * P, :])

        def reserve(k):
            if k not in res_rows:
                load_res(k)
            rows = res_rows[k]
            banks = []
            for c in range(CHUNKS):
                bank = psum.tile([P, BANK], F32, name="sum", tag="sum", bufs=4)
                for b in range(BLOCKS):
                    m0 = c * BANK + b * P
                    nc.tensor.matmul(
                        bank[:, b * P : (b + 1) * P], rows[:, m0 : m0 + P], ident[:],
                        start=(b == 0), stop=False, is_transpose=True,
                    )
                banks.append(bank)
            sums[k] = banks

        z_t = {}

        def quotient(k):
            a, i = divmod(k, TILES_PER_PASS)
            page = pages[0, k % 2]
            for c in range(CHUNKS):
                bank = sums[k][c]
                for b in range(BLOCKS):
                    m0 = c * BANK + b * P
                    nc.tensor.matmul(
                        bank[:, b * P : (b + 1) * P], page[:, m0 : m0 + P], ident[:],
                        start=False, stop=(b == BLOCKS - 1), is_transpose=True,
                    )
                if i == 0:
                    z_t[a, c] = keep.tile([P, BLOCKS * BANK], BF16, name=f"z_t{a}_{c}")
                place = z_t[a, c][:].rearrange("p (b u q e) -> p u b q e", b=BLOCKS, u=2, e=2)
                total = bank[:].rearrange("p (b q u e) -> p u b q e", b=BLOCKS, u=2, e=2)
                engine = nc.vector
                if k + 1 < TILES:
                    held = ring.tile([P, BANK], F32, name="held", bufs=4)
                    ordered = held[:].rearrange("p (u b q e) -> p u b q e", u=2, b=BLOCKS, e=2)
                    if helped(k, c):
                        nc.scalar.activation(ordered, total, ACT.Copy, scale=CENTRE)
                    else:
                        nc.scalar.copy(ordered, total)
                    total, engine = ordered, nc.gpsimd
                engine.tensor_tensor(
                    place[:, :, :, 32 * i : 32 * (i + 1), :],
                    total,
                    damp[k][:, c * BANK : (c + 1) * BANK].rearrange("p (u b q e) -> p u b q e", u=2, b=BLOCKS, e=2),
                    MULT,
                )

        z_q = {}
        z_woven = {}

        def weave_z(a, c, tags, movers):
            pairs = z_t[a, c][:].bitcast(F32)
            woven = ring.tile([P, BANK * PACK], BF16, name="z_woven", bufs=4, align_bytes=64)
            for j in range(2):
                bank = psum.tile([P, BANK], F32, name="back", tag=tags[j])
                for i in range(4):
                    w0 = (4 * j + i) * P
                    nc.tensor.transpose(bank[:, i * P : (i + 1) * P], pairs[:, w0 : w0 + P], ident[:])
                movers[j](
                    woven[:].bitcast(F32)[:, j * BANK : (j + 1) * BANK].rearrange("p (b m u) -> p b m u", b=2, u=2),
                    bank[:].rearrange("p (b u m) -> p b m u", b=2, u=2),
                )
            z_woven[a, c] = woven

        def quantise_z(a, c):
            woven = z_woven[a, c]
            if a == 0:
                codes = reuse.tile([P, BANK], U32, name=f"z_w0_{c}", offset=(28 if c < 2 else 4) * S + 4 * BANK * c, align_bytes=64)
            else:
                codes = keep.tile([P, BANK], U32, name=f"z_w{a}_{c}", align_bytes=64)
            scales = keep.tile([P, BANK], U8, name=f"z_s{a}_{c}", align_bytes=64)
            nc.vector.quantize_mx(out=codes[:].bitcast(FP8X4), scales=scales[:], in_=woven[:])
            z_q[a, c] = (codes, scales)

        accs = {}

        def score_pass(c, n, a, tag):
            if a == 0:
                accs[c, n] = psum.tile([P, BANK], F32, name="score", tag=tag, bufs=4 if tag == "sum" else 2)
            nc.tensor.matmul_mx(
                out=accs[c, n][:],
                lhsT=wo_w[:, a, n * P : (n + 1) * P].bitcast(FP8X4),
                lhsT_scale=wo_s[:, a, n * P : (n + 1) * P],
                rhs=z_q[a, c][0][:].bitcast(FP8X4),
                rhs_scale=z_q[a, c][1][:],
                start=(a == 0),
                stop=(a == PASSES - 1),
            )

        def scores(c, movers):
            for n in range(N // P):
                if (c, n) not in accs:
                    score_pass(c, n, 0, "sum" if n else "h_acc")
            for n in range(N // P):
                score_pass(c, n, 1, None)
                done = ring.tile([P, BANK], F32, name="done", bufs=6)
                movers[n](done[:], accs[c, n][:])
                nc.sync.dma_start(out[n * P : (n + 1) * P, c * BANK : (c + 1) * BANK], done[:])

        act, dve = nc.scalar.copy, nc.vector.tensor_copy
        nc.sync.dma_start(wb_w[:].bitcast(I32), wb_words[0].bitcast(I32))
        for q in range(4):
            nc.sync.dma_start(wb_s[32 * q : 32 * q + 4, :].bitcast(I32), wb_scales[0, 4 * q : 4 * q + 4, :].bitcast(I32))
        nc.sync.dma_start(ask_lots[:], offs3)
        nc.sync.dma_start(gain[1][:], wg2)
        nc.sync.dma_start(bid_lots[:], offs2)
        nc.sync.dma_start(gain[0][:], wg1)
        load_res(0)
        gather(v_s, tab_s)
        gather(v_w, tab_w)
        for c0, width in WA_FIRST:
            quantise_wa(c0, width, first_wa[:, :, c0 : c0 + width])
        pages[1, 1] = reuse.tile([P, T2], F32, name="page11", offset=16 * S, align_bytes=64)
        pages[0, 1] = reuse.tile([P, T2], F32, name="page01", offset=8 * S, align_bytes=64)
        nc.gpsimd.memset(pages[1, 1][:], 0.0)
        features(1, 0)
        scatter(1, 0, pieces=HALVES)
        features(1, 1)
        features(0, 0)
        nc.gpsimd.memset(pages[0, 1][:], 0.0)
        for k in range(TILES):
            last = k + 1 == TILES
            scatter(0, k)
            if last:
                for c in (0, 1):
                    quantise_z(0, c)
            squares(k)
            if not last:
                features(0, k + 1)
            damping(k)
            if not last:
                scatter(1, k + 1)
            reserve(k)
            if k == 0:
                quantise_wa(WA_HALF, WA_HALF, load_wa(WA_HALF, WA_HALF)[:])
            if k == 2:
                nc.sync.dma_start(wo_w[:].bitcast(I32), wo_words.rearrange("a p n i -> p a (n i)").bitcast(I32))
                for q in range(4):
                    nc.sync.dma_start(
                        wo_s[32 * q : 32 * q + 4, :, :].bitcast(I32),
                        wo_scales[:, 4 * q : 4 * q + 4, :].rearrange("a r n -> r a n").bitcast(I32),
                    )
            for c in {4: [0, 1], 5: [2], 6: [3]}.get(k, []):
                weave_z(0, c, ("turned", "turned"), (act, act))
            if k + 2 < TILES:
                features(1, k + 2)
            quotient(k)
        for n in range(2):
            score_pass(0, n, 0, "h_acc")
        weave_z(1, 0, ("turned", "turned"), (act, act))
        quantise_z(1, 0)
        weave_z(1, 1, ("turned", "turned"), (act, dve))
        quantise_z(1, 1)
        quantise_z(0, 2)
        scores(0, (act, dve, act))
        weave_z(1, 2, ("turned", "turned"), (act, dve))
        quantise_z(1, 2)
        quantise_z(0, 3)
        scores(1, (act, dve, act))
        weave_z(1, 3, ("turned", "turned"), (act, dve))
        quantise_z(1, 3)
        scores(2, (act, act, act))
        scores(3, (act, dve, act))
